import numpy as np
import ml_dtypes


def mxq(x, axis, fmt="e4m3"):
    dtype, down = {"e4m3": (ml_dtypes.float8_e4m3fn, 7), "e5m2": (ml_dtypes.float8_e5m2, 14)}[fmt]
    v = np.moveaxis(np.asarray(x, np.float32).astype(ml_dtypes.bfloat16).astype(np.float64), axis, -1)
    blocks = v.reshape(v.shape[:-1] + (-1, 32))
    amax = np.abs(blocks).max(-1, keepdims=True)
    byte = np.maximum(np.where(amax > 0, np.frexp(amax)[1] - 1 + 127, 0) - down, 1)
    scale = np.exp2(byte - 127.0)
    codes = (blocks / scale).astype(np.float32).astype(dtype).astype(np.float64)
    return np.moveaxis((codes * scale).reshape(v.shape), -1, axis)


WIDE = False


def mx_kscale(k):
    if not WIDE:
        return np.ones(k)
    levels = np.array([10, -10, 5, -5, 0])
    if k % 512:
        return np.exp2(np.random.permutation(np.resize(levels, k // 32))).repeat(32)
    a = np.empty((k // 512, 16))
    for p in range(k // 512):
        a[p, :8] = np.random.permutation(np.resize(levels, 8))
        for g in range(8):
            far = levels[np.abs(levels - a[p, g]) >= 10]
            a[p, g + 8] = far[np.random.randint(len(far))]
    return np.exp2(a.ravel()).repeat(32)


def f64(x):
    return np.asarray(x).astype(np.float64)


def striped(idx):
    return np.tile(np.asarray(idx).reshape(-1, 16).T, (8, 1)).astype(np.uint16)


def unstriped(offs):
    return offs[:16].T.reshape(-1).astype(np.int64)


E2M1 = np.array([0.0, 0.5, 1.0, 1.5, 2.0, 3.0, 4.0, 6.0, -0.0, -0.5, -1.0, -1.5, -2.0, -3.0, -4.0, -6.0])


def pack_weight(w, fmt):
    k, n = w.shape
    w = f64(np.asarray(w, np.float32).astype(ml_dtypes.bfloat16)).reshape(k // 32, 32, n)
    amax = np.abs(w).max(1)
    if fmt == "e4m3":
        byte = np.frexp(amax)[1] - 1 + 127 - 7
    else:
        mant, ex = np.frexp(amax / 6.0)
        byte = np.where(mant > 0.5, ex, ex - 1) + 127
    byte = np.clip(np.where(amax > 0, byte, 1), 1, 254)
    scaled = (w * np.exp2(127.0 - byte)[:, None, :]).reshape(k, n).astype(np.float32)
    by_word = np.ascontiguousarray(scaled.reshape(k // 512, 128, 4, n).transpose(0, 1, 3, 2))
    if fmt == "e4m3":
        words = by_word.astype(ml_dtypes.float8_e4m3fn).view(np.uint8)
    else:
        c = by_word.astype(ml_dtypes.float4_e2m1fn).view(np.uint8) & 0xF
        words = (c[..., 0::2] | (c[..., 1::2] << 4)).reshape(k // 512, 128, 2 * n)
    return np.ascontiguousarray(words), np.ascontiguousarray(byte.astype(np.uint8).reshape(k // 512, 16, n))


def unpack_weight(words, scales, fmt):
    g, _, n = scales.shape
    words = np.ascontiguousarray(words).reshape(g, 128, n, -1)
    if fmt == "e4m3":
        vals = words.view(ml_dtypes.float8_e4m3fn).astype(np.float64)
    else:
        nib = np.empty((g, 128, n, 4), np.uint8)
        nib[..., 0::2] = words & 0xF
        nib[..., 1::2] = words >> 4
        vals = E2M1[nib]
    vals = vals * np.repeat(np.exp2(scales.astype(np.float64) - 127.0), 8, axis=1)[..., None]
    return vals.transpose(0, 1, 3, 2).reshape(g * 512, n)


D, T, I, Q, E, M = 512, 2048, 512, 256, 512, 1024


def setup_inputs():
    n = np.random.standard_normal
    idx = np.random.permutation(T)[:I]
    idx2 = np.random.permutation(T)[:I]
    idx3 = np.random.permutation(M)[:Q]
    fd = mx_kscale(D)
    fi = mx_kscale(I)
    ti = np.ones(T)
    ti[idx] = fi
    keysp = pack_weight(n((D, T)) / fd[:, None], "e4m3")
    return {
        "query": (n((D, Q)) * 1.0 / np.sqrt(D) * fd[:, None]).astype(np.float32),
        "keys_words": keysp[0],
        "keys_scales": keysp[1],
        "os": (np.random.uniform(0.02, 0.08, (1, I)) * fi).astype(np.float32),
        "vals": (n((E, T)) / ti).astype(np.float32),
        "member": (n((E, M))).astype(np.float32),
        "offs": striped(idx),
        "offs2": striped(idx2),
        "offs3": striped(idx3),
    }


def reference(query, keys_words, keys_scales, os, vals, member, offs, offs2, offs3):
    idx = unstriped(offs)
    idx2 = unstriped(offs2)
    idx3 = unstriped(offs3)
    keysu = unpack_weight(keys_words, keys_scales, "e4m3")
    queryq = mxq(f64(query), 0, "e4m3")
    a = queryq.T @ keysu
    s = a[:, idx] - a[:, idx2]
    w = np.maximum(s, 0.0)
    wo1 = w * f64(os)
    wt1 = wo1.T
    vt1 = f64(vals)[:, idx].T
    vt1q = mxq(vt1, 0, "e4m3")
    wt1q = mxq(wt1, 0, "e4m3")
    o = vt1q.T @ wt1q
    y = np.abs(o - f64(member)[:, idx3])
    return y

@@ -1,0 +1,209 @@
+from contextlib import ExitStack
+
+import concourse.mybir as mybir
+from concourse.masks import make_identity
+
+D, T, I, Q, E, M = 512, 2048, 512, 256, 512, 1024
+FLOPS = 2 * Q * D * T + 2 * E * I * Q
+
+F32 = mybir.dt.float32
+BF16 = mybir.dt.bfloat16
+I32 = mybir.dt.int32
+U32 = mybir.dt.uint32
+U16 = mybir.dt.uint16
+U8 = mybir.dt.uint8
+FP8X4 = mybir.dt.float8_e4m3fn_x4
+ALU = mybir.AluOpType
+ACT = mybir.ActivationFunctionType
+
+P = 128
+PACK = 4
+BANK = 512
+Q_TILES = Q // P
+E_TILES = E // P
+KEY_CHUNKS = T // BANK
+KEY_LOADS = 2
+
+
+def tile_attend_difference_distanceout_lean_kernel(
+    tc, query, keys_words, keys_scales, slot_factor, vals, member, offs, offs2, offs3, out
+):
+    nc = tc.nc
+    with ExitStack() as ctx:
+        keep = ctx.enter_context(tc.tile_pool(name="keep", bufs=1))
+        acc_pool = ctx.enter_context(tc.psum_pool(name="acc", bufs=4))
+        turn_pool = ctx.enter_context(tc.psum_pool(name="turn", bufs=3))
+        os_pool = ctx.enter_context(tc.psum_pool(name="osbank", bufs=1))
+
+        def sb(name, shape, dtype):
+            return keep.tile(shape, dtype, name=name, align_bytes=64)
+
+        key_scales = sb("key_scales", [P, BANK], U8)
+        nc.vector.memset(key_scales[:].bitcast(I32), 0)
+        scale_rows = keys_scales[0].bitcast(I32)
+        landed = sb("landed_scales", [P, BANK // 4], I32)
+        for quad in range(4):
+            nc.scalar.dma_start(
+                out=landed[32 * quad : 32 * quad + 16, :],
+                in_=scale_rows[4 * quad : 4 * quad + 4, :].rearrange("r (c n) -> c r n", c=KEY_CHUNKS),
+            )
+        for quad in range(4):
+            live = slice(32 * quad, 32 * quad + 16)
+            nc.vector.tensor_copy(out=key_scales[live, :].bitcast(I32), in_=landed[live, :])
+
+        q_raw = sb("q_raw", [P, PACK, Q], F32)
+        nc.sync.dma_start(out=q_raw[:], in_=query.rearrange("(p t) q -> p t q", t=PACK))
+
+        words = keys_words[0].rearrange("p n t -> p (n t)").bitcast(I32)
+        load_w = T // KEY_LOADS
+        key_codes = []
+        for h in range(KEY_LOADS):
+            codes = sb(f"key_codes{h}", [P, load_w], U32)
+            nc.sync.dma_start(out=codes[:].bitcast(I32), in_=words[:, h * load_w : (h + 1) * load_w])
+            key_codes.append(codes)
+
+        list2 = keep.tile([P, I // 16], U16, name="list2")
+        nc.sync.dma_start(list2[:], offs2)
+        list1 = keep.tile([P, I // 16], U16, name="list1")
+        nc.sync.dma_start(list1[:], offs)
+        os_cols = sb("os_cols", [P, PACK], F32)
+        nc.sync.dma_start(out=os_cols[:], in_=slot_factor.rearrange("o (p t) -> (o p) t", t=PACK))
+
+        val_rows = []
+        for j in range(E_TILES):
+            rows = sb(f"val_rows{j}", [P, T], F32)
+            nc.sync.dma_start(out=rows[:], in_=vals[j * P : (j + 1) * P, :])
+            val_rows.append(rows)
+        list3 = keep.tile([P, Q // 16], U16, name="list3")
+        nc.sync.dma_start(list3[:], offs3)
+        member_rows = []
+        for j in range(E_TILES):
+            rows = sb(f"member_rows{j}", [P, M], F32)
+            nc.sync.dma_start(out=rows[:], in_=member[j * P : (j + 1) * P, :])
+            member_rows.append(rows)
+
+        ident = sb("ident", [P, P], F32)
+        make_identity(nc, ident[:])
+
+        q_codes, q_scales, q_woven = [], [], []
+        for h in range(Q_TILES):
+            woven = sb(f"q_woven{h}", [P, P, PACK], BF16)
+            src = q_raw[:, :, h * P : (h + 1) * P].rearrange("p t (c x) -> p c t x", x=4)
+            dst = woven[:].rearrange("p (c x) t -> p c t x", x=4)
+            if h == 0:
+                nc.vector.tensor_copy(out=dst, in_=src)
+            else:
+                nc.scalar.activation(out=dst, in_=src, func=ACT.Copy)
+            q_woven.append(woven)
+        for h in range(Q_TILES):
+            codes = sb(f"q_codes{h}", [P, P], U32)
+            scales = sb(f"q_scales{h}", [P, P], U8)
+            nc.vector.quantize_mx(
+                out=codes[:].bitcast(FP8X4), scales=scales[:], in_=q_woven[h][:].rearrange("p q t -> p (q t)")
+            )
+            q_codes.append(codes)
+            q_scales.append(scales)
+
+        scores = [sb(f"scores{h}", [P, T], F32) for h in range(Q_TILES)]
+        per_load = KEY_CHUNKS // KEY_LOADS
+        for c in range(KEY_CHUNKS):
+            moving = key_codes[c // per_load][:, (c % per_load) * BANK : (c % per_load + 1) * BANK]
+            for h in range(Q_TILES):
+                acc = acc_pool.tile([P, BANK], F32, name="acc")
+                nc.tensor.matmul_mx(
+                    out=acc[:],
+                    lhsT=q_codes[h][:].bitcast(FP8X4),
+                    lhsT_scale=q_scales[h][:],
+                    rhs=moving.bitcast(FP8X4),
+                    rhs_scale=key_scales[4 * c : P, :],
+                    start=True,
+                    stop=True,
+                )
+                dst = scores[h][:, c * BANK : (c + 1) * BANK]
+                if h == 0:
+                    nc.vector.tensor_copy(out=dst, in_=acc[:])
+                else:
+                    nc.scalar.copy(out=dst, in_=acc[:])
+
+        os_bank = os_pool.tile([P, PACK, P], F32, name="os_bank")
+        for t in range(PACK):
+            nc.tensor.transpose(os_bank[:, t, :], os_cols[:, t : t + 1].to_broadcast([P, P]), ident[:])
+
+        def turn(rows_bf16, woven_words, engine_copy):
+            pairs = rows_bf16.bitcast(F32)
+            bank = turn_pool.tile([P, 2, P], F32, name="turn")
+            for u in range(2):
+                nc.tensor.transpose(bank[:, u, :], pairs[:, u::2], ident[:])
+            engine_copy(out=woven_words, in_=bank[:].rearrange("p u r -> p r u"))
+
+        second = [sb(f"second{h}", [P, I], F32) for h in range(Q_TILES)]
+        nc.vector.tensor_copy(out=second[0][:], in_=scores[0][:].indirect(list2[:]))
+        nc.scalar.activation(out=second[1][:], in_=scores[1][:].indirect(list2[:]), func=ACT.Copy)
+        w_codes = sb("w_codes", [P, Q], U32)
+        w_scales = sb("w_scales", [P, Q], U8)
+        diffs = []
+        for h in range(Q_TILES):
+            diff = sb(f"diff{h}", [P, I], F32)
+            nc.vector.tensor_tensor(diff[:], scores[h][:].indirect(list1[:]), second[h][:], ALU.subtract)
+            diffs.append(diff)
+
+        def as_words(woven):
+            return woven[:].bitcast(F32).rearrange("p (r u) -> p r u", u=2)
+
+        def weigh(h, buffer_tag):
+            w_rows = keep.tile([P, I], BF16, name=f"w_rows{h}", tag=buffer_tag, align_bytes=64)
+            nc.vector.scalar_tensor_tensor(
+                out=w_rows[:].rearrange("q (p t) -> q p t", t=PACK),
+                in0=diffs[h][:].rearrange("q (p t) -> q p t", t=PACK),
+                scalar=0.0,
+                in1=os_bank[:].rearrange("q t p -> q p t"),
+                op0=ALU.max,
+                op1=ALU.mult,
+            )
+            return w_rows
+
+        def turn_and_quantise(name, rows, codes, scales):
+            woven = sb(name, [P, P * PACK], BF16)
+            turn(rows[:], as_words(woven), nc.vector.tensor_copy)
+            nc.vector.quantize_mx(out=codes.bitcast(FP8X4), scales=scales, in_=woven[:])
+
+        v_codes = [sb(f"v_codes{j}", [P, P], U32) for j in range(E_TILES)]
+        v_scales = [sb(f"v_scales{j}", [P, P], U8) for j in range(E_TILES)]
+        weights_after = {0: 0, 2: 1}
+        for j in range(E_TILES):
+            v_rows = keep.tile([P, I], BF16, name=f"v_rows{j}", tag=f"rows{j}", align_bytes=64)
+            nc.scalar.activation(out=v_rows[:], in_=val_rows[j][:].indirect(list1[:]), func=ACT.Copy)
+            woven = sb(f"v_woven{j}", [P, P * PACK], BF16)
+            pairs = v_rows[:].bitcast(F32)
+            bank = turn_pool.tile([P, 2, P], F32, name="turn")
+            for u in range(2):
+                nc.tensor.transpose(bank[:, u, :], pairs[:, u::2], ident[:])
+            if j in weights_after:
+                w_rows = weigh(weights_after[j], f"rows{j}")
+            nc.vector.tensor_copy(out=as_words(woven), in_=bank[:].rearrange("p u r -> p r u"))
+            nc.vector.quantize_mx(out=v_codes[j][:].bitcast(FP8X4), scales=v_scales[j][:], in_=woven[:])
+            if j in weights_after:
+                h = weights_after[j]
+                cols = slice(h * P, (h + 1) * P)
+                turn_and_quantise(f"w_woven{h}", w_rows, w_codes[:, cols], w_scales[:, cols])
+
+        sums = keep.tile([P, E_TILES, Q], F32, name="sums", tag=f"rows{E_TILES - 1}", align_bytes=64)
+        for j in range(E_TILES):
+            acc = acc_pool.tile([P, BANK], F32, name="acc")
+            nc.tensor.matmul_mx(
+                out=acc[:, 0:Q],
+                lhsT=v_codes[j][:].bitcast(FP8X4),
+                lhsT_scale=v_scales[j][:],
+                rhs=w_codes[:].bitcast(FP8X4),
+                rhs_scale=w_scales[:],
+                start=True,
+                stop=True,
+            )
+            nc.scalar.copy(out=sums[:, j, :], in_=acc[:, 0:Q])
+
+        for j in range(E_TILES):
+            gap = sb(f"gap{j}", [P, Q], F32)
+            nc.vector.tensor_tensor(gap[:], member_rows[j][:].indirect(list3[:]), sums[:, j, :], ALU.subtract)
+            dist = sb(f"dist{j}", [P, Q], F32)
+            nc.scalar.activation(out=dist[:], in_=gap[:], func=ACT.Abs)
+            nc.scalar.dma_start(out=out[j * P : (j + 1) * P, :], in_=dist[:])

@@ -22,7 +22,7 @@ BANK = 512
 Q_TILES = Q // P
 E_TILES = E // P
 KEY_CHUNKS = T // BANK
-KEY_LOADS = 2
+KEY_LOADS = (512, 512, 1024)
 
 
 def tile_attend_difference_distanceout_lean_kernel(
@@ -33,41 +33,37 @@ def tile_attend_difference_distanceout_lean_kernel(
         keep = ctx.enter_context(tc.tile_pool(name="keep", bufs=1))
         acc_pool = ctx.enter_context(tc.psum_pool(name="acc", bufs=4))
         turn_pool = ctx.enter_context(tc.psum_pool(name="turn", bufs=3))
-        os_pool = ctx.enter_context(tc.psum_pool(name="osbank", bufs=1))
+        factor_pool = ctx.enter_context(tc.psum_pool(name="factor", bufs=1))
 
-        def sb(name, shape, dtype):
-            return keep.tile(shape, dtype, name=name, align_bytes=64)
-
-        key_scales = sb("key_scales", [P, BANK], U8)
-        nc.vector.memset(key_scales[:].bitcast(I32), 0)
-        scale_rows = keys_scales[0].bitcast(I32)
-        landed = sb("landed_scales", [P, BANK // 4], I32)
-        for quad in range(4):
-            nc.scalar.dma_start(
-                out=landed[32 * quad : 32 * quad + 16, :],
-                in_=scale_rows[4 * quad : 4 * quad + 4, :].rearrange("r (c n) -> c r n", c=KEY_CHUNKS),
-            )
-        for quad in range(4):
-            live = slice(32 * quad, 32 * quad + 16)
-            nc.vector.tensor_copy(out=key_scales[live, :].bitcast(I32), in_=landed[live, :])
+        def sb(name, shape, dtype, tag=None):
+            return keep.tile(shape, dtype, name=name, tag=tag or name, align_bytes=64)
 
         q_raw = sb("q_raw", [P, PACK, Q], F32)
         nc.sync.dma_start(out=q_raw[:], in_=query.rearrange("(p t) q -> p t q", t=PACK))
 
+        scale_rows = keys_scales[0].bitcast(I32)
+        landed = sb("landed_scales", [P, BANK // 4], I32)
+        for quad in range(4):
+            nc.sync.dma_start(
+                out=landed[32 * quad : 32 * quad + 16, :],
+                in_=scale_rows[4 * quad : 4 * quad + 4, :].rearrange("r (c n) -> c r n", c=KEY_CHUNKS),
+            )
+
         words = keys_words[0].rearrange("p n t -> p (n t)").bitcast(I32)
-        load_w = T // KEY_LOADS
-        key_codes = []
-        for h in range(KEY_LOADS):
-            codes = sb(f"key_codes{h}", [P, load_w], U32)
-            nc.sync.dma_start(out=codes[:].bitcast(I32), in_=words[:, h * load_w : (h + 1) * load_w])
-            key_codes.append(codes)
+        key_chunks = []
+        first = 0
+        for width in KEY_LOADS:
+            codes = sb(f"key_codes{first}", [P, width], U32)
+            nc.sync.dma_start(out=codes[:].bitcast(I32), in_=words[:, first : first + width])
+            key_chunks.extend(codes[:, c : c + BANK] for c in range(0, width, BANK))
+            first = first + width
 
         list2 = keep.tile([P, I // 16], U16, name="list2")
         nc.sync.dma_start(list2[:], offs2)
         list1 = keep.tile([P, I // 16], U16, name="list1")
         nc.sync.dma_start(list1[:], offs)
-        os_cols = sb("os_cols", [P, PACK], F32)
-        nc.sync.dma_start(out=os_cols[:], in_=slot_factor.rearrange("o (p t) -> (o p) t", t=PACK))
+        factor_cols = sb("factor_cols", [P, PACK], F32)
+        nc.sync.dma_start(out=factor_cols[:], in_=slot_factor.rearrange("o (p t) -> (o p) t", t=PACK))
 
         val_rows = []
         for j in range(E_TILES):
@@ -82,10 +78,12 @@ def tile_attend_difference_distanceout_lean_kernel(
             nc.sync.dma_start(out=rows[:], in_=member[j * P : (j + 1) * P, :])
             member_rows.append(rows)
 
+        key_scales = sb("key_scales", [P, BANK], U8)
+        nc.vector.memset(key_scales[:].bitcast(I32), 0)
         ident = sb("ident", [P, P], F32)
         make_identity(nc, ident[:])
 
-        q_codes, q_scales, q_woven = [], [], []
+        q_woven = []
         for h in range(Q_TILES):
             woven = sb(f"q_woven{h}", [P, P, PACK], BF16)
             src = q_raw[:, :, h * P : (h + 1) * P].rearrange("p t (c x) -> p c t x", x=4)
@@ -95,6 +93,10 @@ def tile_attend_difference_distanceout_lean_kernel(
             else:
                 nc.scalar.activation(out=dst, in_=src, func=ACT.Copy)
             q_woven.append(woven)
+        for quad in range(4):
+            live = slice(32 * quad, 32 * quad + 16)
+            nc.vector.tensor_copy(out=key_scales[live, :].bitcast(I32), in_=landed[live, :])
+        q_codes, q_scales = [], []
         for h in range(Q_TILES):
             codes = sb(f"q_codes{h}", [P, P], U32)
             scales = sb(f"q_scales{h}", [P, P], U8)
@@ -105,105 +107,121 @@ def tile_attend_difference_distanceout_lean_kernel(
             q_scales.append(scales)
 
         scores = [sb(f"scores{h}", [P, T], F32) for h in range(Q_TILES)]
-        per_load = KEY_CHUNKS // KEY_LOADS
-        for c in range(KEY_CHUNKS):
-            moving = key_codes[c // per_load][:, (c % per_load) * BANK : (c % per_load + 1) * BANK]
-            for h in range(Q_TILES):
+        for h in range(Q_TILES):
+            for c in range(KEY_CHUNKS):
                 acc = acc_pool.tile([P, BANK], F32, name="acc")
                 nc.tensor.matmul_mx(
                     out=acc[:],
                     lhsT=q_codes[h][:].bitcast(FP8X4),
                     lhsT_scale=q_scales[h][:],
-                    rhs=moving.bitcast(FP8X4),
+                    rhs=key_chunks[c].bitcast(FP8X4),
                     rhs_scale=key_scales[4 * c : P, :],
                     start=True,
                     stop=True,
                 )
                 dst = scores[h][:, c * BANK : (c + 1) * BANK]
-                if h == 0:
+                if (h, c) in ((0, 1), (0, 3), (1, 1)):
                     nc.vector.tensor_copy(out=dst, in_=acc[:])
                 else:
                     nc.scalar.copy(out=dst, in_=acc[:])
 
-        os_bank = os_pool.tile([P, PACK, P], F32, name="os_bank")
+        factor_bank = factor_pool.tile([P, PACK, P], F32, name="factor_bank")
         for t in range(PACK):
-            nc.tensor.transpose(os_bank[:, t, :], os_cols[:, t : t + 1].to_broadcast([P, P]), ident[:])
+            nc.tensor.transpose(factor_bank[:, t, :], factor_cols[:, t : t + 1].to_broadcast([P, P]), ident[:])
 
-        def turn(rows_bf16, woven_words, engine_copy):
-            pairs = rows_bf16.bitcast(F32)
+        def turn(rows):
+            pairs = rows[:].bitcast(F32)
             bank = turn_pool.tile([P, 2, P], F32, name="turn")
             for u in range(2):
                 nc.tensor.transpose(bank[:, u, :], pairs[:, u::2], ident[:])
-            engine_copy(out=woven_words, in_=bank[:].rearrange("p u r -> p r u"))
+            return bank
 
-        second = [sb(f"second{h}", [P, I], F32) for h in range(Q_TILES)]
-        nc.vector.tensor_copy(out=second[0][:], in_=scores[0][:].indirect(list2[:]))
-        nc.scalar.activation(out=second[1][:], in_=scores[1][:].indirect(list2[:]), func=ACT.Copy)
-        w_codes = sb("w_codes", [P, Q], U32)
-        w_scales = sb("w_scales", [P, Q], U8)
-        diffs = []
-        for h in range(Q_TILES):
+        def weave(copy, bank, woven):
+            copy(out=woven.bitcast(F32).rearrange("p (r u) -> p r u", u=2), in_=bank[:].rearrange("p u r -> p r u"))
+
+        def quantise(name, woven, tag=None):
+            width = woven.shape[1] // PACK
+            codes = sb(f"{name}_codes", [P, width], U32, tag=tag)
+            scales = sb(f"{name}_scales", [P, width], U8)
+            nc.vector.quantize_mx(out=codes[:].bitcast(FP8X4), scales=scales[:], in_=woven[:])
+            return codes, scales
+
+        def gather_values(j):
+            rows = sb(f"v_rows{j}", [P, I], BF16)
+            nc.scalar.activation(out=rows[:], in_=val_rows[j][:].indirect(list1[:]), func=ACT.Copy)
+            return rows
+
+        def difference(h):
             diff = sb(f"diff{h}", [P, I], F32)
             nc.vector.tensor_tensor(diff[:], scores[h][:].indirect(list1[:]), second[h][:], ALU.subtract)
-            diffs.append(diff)
+            return diff
 
-        def as_words(woven):
-            return woven[:].bitcast(F32).rearrange("p (r u) -> p r u", u=2)
-
-        def weigh(h, buffer_tag):
-            w_rows = keep.tile([P, I], BF16, name=f"w_rows{h}", tag=buffer_tag, align_bytes=64)
+        def weigh(h, diff, tag=None):
+            rows = sb(f"w_rows{h}", [P, I], BF16, tag=tag)
             nc.vector.scalar_tensor_tensor(
-                out=w_rows[:].rearrange("q (p t) -> q p t", t=PACK),
-                in0=diffs[h][:].rearrange("q (p t) -> q p t", t=PACK),
+                out=rows[:].rearrange("q (p t) -> q p t", t=PACK),
+                in0=diff[:].rearrange("q (p t) -> q p t", t=PACK),
                 scalar=0.0,
-                in1=os_bank[:].rearrange("q t p -> q p t"),
+                in1=factor_bank[:].rearrange("q t p -> q p t"),
                 op0=ALU.max,
                 op1=ALU.mult,
             )
-            return w_rows
+            return rows
 
-        def turn_and_quantise(name, rows, codes, scales):
-            woven = sb(name, [P, P * PACK], BF16)
-            turn(rows[:], as_words(woven), nc.vector.tensor_copy)
-            nc.vector.quantize_mx(out=codes.bitcast(FP8X4), scales=scales, in_=woven[:])
+        W = P * PACK
+        early_woven = sb("early_woven", [P, 2 * W], BF16)
+        late_woven = sb("late_woven", [P, 3 * W], BF16)
+        second = [sb(f"second{h}", [P, I], F32) for h in range(Q_TILES)]
+        nc.vector.tensor_copy(out=second[0][:], in_=scores[0][:].indirect(list2[:]))
+        nc.scalar.activation(out=second[1][:], in_=scores[1][:].indirect(list2[:]), func=ACT.Copy)
 
-        v_codes = [sb(f"v_codes{j}", [P, P], U32) for j in range(E_TILES)]
-        v_scales = [sb(f"v_scales{j}", [P, P], U8) for j in range(E_TILES)]
-        weights_after = {0: 0, 2: 1}
-        for j in range(E_TILES):
-            v_rows = keep.tile([P, I], BF16, name=f"v_rows{j}", tag=f"rows{j}", align_bytes=64)
-            nc.scalar.activation(out=v_rows[:], in_=val_rows[j][:].indirect(list1[:]), func=ACT.Copy)
-            woven = sb(f"v_woven{j}", [P, P * PACK], BF16)
-            pairs = v_rows[:].bitcast(F32)
-            bank = turn_pool.tile([P, 2, P], F32, name="turn")
-            for u in range(2):
-                nc.tensor.transpose(bank[:, u, :], pairs[:, u::2], ident[:])
-            if j in weights_after:
-                w_rows = weigh(weights_after[j], f"rows{j}")
-            nc.vector.tensor_copy(out=as_words(woven), in_=bank[:].rearrange("p u r -> p r u"))
-            nc.vector.quantize_mx(out=v_codes[j][:].bitcast(FP8X4), scales=v_scales[j][:], in_=woven[:])
-            if j in weights_after:
-                h = weights_after[j]
-                cols = slice(h * P, (h + 1) * P)
-                turn_and_quantise(f"w_woven{h}", w_rows, w_codes[:, cols], w_scales[:, cols])
+        w_bank0 = turn(weigh(0, difference(0)))
+        diff1 = difference(1)
+        weave(nc.vector.tensor_copy, w_bank0, late_woven[:, 0:W])
+        weave(nc.vector.tensor_copy, turn(gather_values(0)), early_woven[:, 0:W])
+        v_bank1 = turn(gather_values(1))
+        w_rows1 = weigh(1, diff1, tag="v_rows1")
+        weave(nc.vector.tensor_copy, v_bank1, early_woven[:, W : 2 * W])
+        weave(nc.vector.tensor_copy, turn(w_rows1), late_woven[:, W : 2 * W])
+        early_codes, early_scales = quantise("early", early_woven)
+        weave(nc.vector.tensor_copy, turn(gather_values(2)), late_woven[:, 2 * W : 3 * W])
+        v_bank3 = turn(gather_values(3))
+        late_codes, late_scales = quantise("late", late_woven, tag="v_rows3")
 
-        sums = keep.tile([P, E_TILES, Q], F32, name="sums", tag=f"rows{E_TILES - 1}", align_bytes=64)
+        def gather_members(j):
+            picked = sb(f"picked{j}", [P, Q], F32)
+            nc.scalar.activation(out=picked[:], in_=member_rows[j][:].indirect(list3[:]), func=ACT.Copy)
+            return picked
+
+        picked = [gather_members(0)]
+        last_woven = sb("last_woven", [P, W], BF16, tag="member_rows0")
+        weave(nc.scalar.copy, v_bank3, last_woven[:])
+        last_codes, last_scales = quantise("last", last_woven)
+        picked.append(gather_members(1))
+        picked.append(gather_members(2))
+        v_codes = [early_codes[:, 0:P], early_codes[:, P : 2 * P], late_codes[:, Q : Q + P], last_codes[:]]
+        v_scales = [early_scales[:, 0:P], early_scales[:, P : 2 * P], late_scales[:, Q : Q + P], last_scales[:]]
+
+        gaps = sb("gaps", [P, E_TILES, Q], F32)
+        dist = sb("dist", [P, E_TILES, Q], F32, tag="member_rows2")
         for j in range(E_TILES):
             acc = acc_pool.tile([P, BANK], F32, name="acc")
             nc.tensor.matmul_mx(
                 out=acc[:, 0:Q],
-                lhsT=v_codes[j][:].bitcast(FP8X4),
-                lhsT_scale=v_scales[j][:],
-                rhs=w_codes[:].bitcast(FP8X4),
-                rhs_scale=w_scales[:],
+                lhsT=v_codes[j].bitcast(FP8X4),
+                lhsT_scale=v_scales[j],
+                rhs=late_codes[:, 0:Q].bitcast(FP8X4),
+                rhs_scale=late_scales[:, 0:Q],
                 start=True,
                 stop=True,
             )
-            nc.scalar.copy(out=sums[:, j, :], in_=acc[:, 0:Q])
+            if j < E_TILES - 1:
+                nc.vector.tensor_tensor(gaps[:, j, :], acc[:, 0:Q], picked[j][:], ALU.subtract)
+            else:
+                nc.scalar.copy(out=dist[:, j, :], in_=acc[:, 0:Q])
+                nc.vector.tensor_tensor(gaps[:, j, :], member_rows[j][:].indirect(list3[:]), dist[:, j, :], ALU.subtract)
 
-        for j in range(E_TILES):
-            gap = sb(f"gap{j}", [P, Q], F32)
-            nc.vector.tensor_tensor(gap[:], member_rows[j][:].indirect(list3[:]), sums[:, j, :], ALU.subtract)
-            dist = sb(f"dist{j}", [P, Q], F32)
-            nc.scalar.activation(out=dist[:], in_=gap[:], func=ACT.Abs)
-            nc.scalar.dma_start(out=out[j * P : (j + 1) * P, :], in_=dist[:])
+        out_tiles = out.rearrange("(j p) q -> p j q", p=P)
+        for tiles, queue in ((slice(0, 2), nc.sync), (slice(2, 3), nc.sync), (slice(3, 4), nc.scalar)):
+            nc.scalar.activation(out=dist[:, tiles, :], in_=gaps[:, tiles, :], func=ACT.Abs)
+            queue.dma_start(out=out_tiles[:, tiles, :], in_=dist[:, tiles, :])

@@ -32,8 +32,7 @@ def tile_attend_difference_distanceout_lean_kernel(
     with ExitStack() as ctx:
         keep = ctx.enter_context(tc.tile_pool(name="keep", bufs=1))
         acc_pool = ctx.enter_context(tc.psum_pool(name="acc", bufs=4))
-        turn_pool = ctx.enter_context(tc.psum_pool(name="turn", bufs=3))
-        factor_pool = ctx.enter_context(tc.psum_pool(name="factor", bufs=1))
+        turn_pool = ctx.enter_context(tc.psum_pool(name="turn", bufs=4))
 
         def sb(name, shape, dtype, tag=None):
             return keep.tile(shape, dtype, name=name, tag=tag or name, align_bytes=64)
@@ -72,11 +71,10 @@ def tile_attend_difference_distanceout_lean_kernel(
             val_rows.append(rows)
         list3 = keep.tile([P, Q // 16], U16, name="list3")
         nc.sync.dma_start(list3[:], offs3)
-        member_rows = []
-        for j in range(E_TILES):
-            rows = sb(f"member_rows{j}", [P, M], F32)
-            nc.sync.dma_start(out=rows[:], in_=member[j * P : (j + 1) * P, :])
-            member_rows.append(rows)
+        member_rows = {}
+        for j in (1, 2, 3, 0):
+            member_rows[j] = sb(f"member_rows{j}", [P, M], F32)
+            nc.sync.dma_start(out=member_rows[j][:], in_=member[j * P : (j + 1) * P, :])
 
         key_scales = sb("key_scales", [P, BANK], U8)
         nc.vector.memset(key_scales[:].bitcast(I32), 0)
@@ -120,12 +118,12 @@ def tile_attend_difference_distanceout_lean_kernel(
                     stop=True,
                 )
                 dst = scores[h][:, c * BANK : (c + 1) * BANK]
-                if (h, c) in ((0, 1), (0, 3), (1, 1)):
+                if c % 2 == 1:
                     nc.vector.tensor_copy(out=dst, in_=acc[:])
                 else:
                     nc.scalar.copy(out=dst, in_=acc[:])
 
-        factor_bank = factor_pool.tile([P, PACK, P], F32, name="factor_bank")
+        factor_bank = acc_pool.tile([P, PACK, P], F32, name="factor_bank", tag="acc")
         for t in range(PACK):
             nc.tensor.transpose(factor_bank[:, t, :], factor_cols[:, t : t + 1].to_broadcast([P, P]), ident[:])
 
@@ -169,41 +167,44 @@ def tile_attend_difference_distanceout_lean_kernel(
             return rows
 
         W = P * PACK
+        second0 = sb("second0", [P, I], F32)
+        nc.vector.tensor_copy(out=second0[:], in_=scores[0][:].indirect(list2[:]))
+        v_bank0 = turn(gather_values(0))
+        second1 = sb("second1", [P, I], F32, tag="val_rows0")
+        nc.scalar.activation(out=second1[:], in_=scores[1][:].indirect(list2[:]), func=ACT.Copy)
+        second = [second0, second1]
+
         early_woven = sb("early_woven", [P, 2 * W], BF16)
         late_woven = sb("late_woven", [P, 3 * W], BF16)
-        second = [sb(f"second{h}", [P, I], F32) for h in range(Q_TILES)]
-        nc.vector.tensor_copy(out=second[0][:], in_=scores[0][:].indirect(list2[:]))
-        nc.scalar.activation(out=second[1][:], in_=scores[1][:].indirect(list2[:]), func=ACT.Copy)
-
-        w_bank0 = turn(weigh(0, difference(0)))
+        diff0 = difference(0)
+        weave(nc.vector.tensor_copy, v_bank0, early_woven[:, 0:W])
+        w_bank0 = turn(weigh(0, diff0, tag="v_rows0"))
         diff1 = difference(1)
         weave(nc.vector.tensor_copy, w_bank0, late_woven[:, 0:W])
-        weave(nc.vector.tensor_copy, turn(gather_values(0)), early_woven[:, 0:W])
         v_bank1 = turn(gather_values(1))
-        w_rows1 = weigh(1, diff1, tag="v_rows1")
+        w_bank1 = turn(weigh(1, diff1, tag="v_rows1"))
         weave(nc.vector.tensor_copy, v_bank1, early_woven[:, W : 2 * W])
-        weave(nc.vector.tensor_copy, turn(w_rows1), late_woven[:, W : 2 * W])
-        early_codes, early_scales = quantise("early", early_woven)
+        weave(nc.vector.tensor_copy, w_bank1, late_woven[:, W : 2 * W])
         weave(nc.vector.tensor_copy, turn(gather_values(2)), late_woven[:, 2 * W : 3 * W])
+        early_codes, early_scales = quantise("early", early_woven, tag="v_rows2")
         v_bank3 = turn(gather_values(3))
-        late_codes, late_scales = quantise("late", late_woven, tag="v_rows3")
+        late_codes, late_scales = quantise("late", late_woven, tag="val_rows3")
 
         def gather_members(j):
             picked = sb(f"picked{j}", [P, Q], F32)
             nc.scalar.activation(out=picked[:], in_=member_rows[j][:].indirect(list3[:]), func=ACT.Copy)
             return picked
 
-        picked = [gather_members(0)]
-        last_woven = sb("last_woven", [P, W], BF16, tag="member_rows0")
-        weave(nc.scalar.copy, v_bank3, last_woven[:])
-        last_codes, last_scales = quantise("last", last_woven)
-        picked.append(gather_members(1))
-        picked.append(gather_members(2))
-        v_codes = [early_codes[:, 0:P], early_codes[:, P : 2 * P], late_codes[:, Q : Q + P], last_codes[:]]
-        v_scales = [early_scales[:, 0:P], early_scales[:, P : 2 * P], late_scales[:, Q : Q + P], last_scales[:]]
+        picked = {1: gather_members(1)}
+        v_woven3 = sb("v_woven3", [P, W], BF16, tag="member_rows1")
+        weave(nc.scalar.copy, v_bank3, v_woven3[:])
+        v_mx3 = quantise("v3", v_woven3)
+        picked[2] = gather_members(2)
+        picked[3] = gather_members(3)
+        v_codes = [early_codes[:, 0:P], early_codes[:, P : 2 * P], late_codes[:, Q : Q + P], v_mx3[0][:]]
+        v_scales = [early_scales[:, 0:P], early_scales[:, P : 2 * P], late_scales[:, Q : Q + P], v_mx3[1][:]]
 
-        gaps = sb("gaps", [P, E_TILES, Q], F32)
-        dist = sb("dist", [P, E_TILES, Q], F32, tag="member_rows2")
+        gaps = sb("gaps", [P, E_TILES + 1, Q], F32, tag="member_rows1")
         for j in range(E_TILES):
             acc = acc_pool.tile([P, BANK], F32, name="acc")
             nc.tensor.matmul_mx(
@@ -215,13 +216,14 @@ def tile_attend_difference_distanceout_lean_kernel(
                 start=True,
                 stop=True,
             )
-            if j < E_TILES - 1:
-                nc.vector.tensor_tensor(gaps[:, j, :], acc[:, 0:Q], picked[j][:], ALU.subtract)
+            if j == 0:
+                nc.vector.tensor_copy(out=gaps[:, E_TILES, :], in_=acc[:, 0:Q])
             else:
-                nc.scalar.copy(out=dist[:, j, :], in_=acc[:, 0:Q])
-                nc.vector.tensor_tensor(gaps[:, j, :], member_rows[j][:].indirect(list3[:]), dist[:, j, :], ALU.subtract)
+                nc.vector.tensor_tensor(gaps[:, j, :], acc[:, 0:Q], picked[j][:], ALU.subtract)
+        nc.vector.tensor_tensor(gaps[:, 0, :], member_rows[0][:].indirect(list3[:]), gaps[:, E_TILES, :], ALU.subtract)
 
+        dist = sb("dist", [P, E_TILES, Q], F32, tag="member_rows3")
         out_tiles = out.rearrange("(j p) q -> p j q", p=P)
-        for tiles, queue in ((slice(0, 2), nc.sync), (slice(2, 3), nc.sync), (slice(3, 4), nc.scalar)):
+        for tiles, queue in ((slice(1, 3), nc.sync), (slice(3, 4), nc.sync), (slice(0, 1), nc.scalar)):
             nc.scalar.activation(out=dist[:, tiles, :], in_=gaps[:, tiles, :], func=ACT.Abs)
             queue.dma_start(out=out_tiles[:, tiles, :], in_=dist[:, tiles, :])

from contextlib import ExitStack

import concourse.mybir as mybir
from concourse.masks import make_identity

D, T, I, Q, E, M = 512, 2048, 512, 256, 512, 1024
FLOPS = 2 * Q * D * T + 2 * E * I * Q

F32 = mybir.dt.float32
BF16 = mybir.dt.bfloat16
I32 = mybir.dt.int32
U32 = mybir.dt.uint32
U16 = mybir.dt.uint16
U8 = mybir.dt.uint8
FP8X4 = mybir.dt.float8_e4m3fn_x4
ALU = mybir.AluOpType
ACT = mybir.ActivationFunctionType

P = 128
PACK = 4
BANK = 512
Q_TILES = Q // P
E_TILES = E // P
KEY_CHUNKS = T // BANK
KEY_LOADS = (512, 512, 1024)


def tile_attend_difference_distanceout_lean_kernel(
    tc, query, keys_words, keys_scales, slot_factor, vals, member, offs, offs2, offs3, out
):
    nc = tc.nc
    with ExitStack() as ctx:
        keep = ctx.enter_context(tc.tile_pool(name="keep", bufs=1))
        acc_pool = ctx.enter_context(tc.psum_pool(name="acc", bufs=4))
        turn_pool = ctx.enter_context(tc.psum_pool(name="turn", bufs=4))

        def sb(name, shape, dtype, tag=None):
            return keep.tile(shape, dtype, name=name, tag=tag or name, align_bytes=64)

        q_raw = sb("q_raw", [P, PACK, Q], F32)
        nc.sync.dma_start(out=q_raw[:], in_=query.rearrange("(p t) q -> p t q", t=PACK))

        scale_rows = keys_scales[0].bitcast(I32)
        landed = sb("landed_scales", [P, BANK // 4], I32)
        for quad in range(4):
            nc.sync.dma_start(
                out=landed[32 * quad : 32 * quad + 16, :],
                in_=scale_rows[4 * quad : 4 * quad + 4, :].rearrange("r (c n) -> c r n", c=KEY_CHUNKS),
            )

        words = keys_words[0].rearrange("p n t -> p (n t)").bitcast(I32)
        key_chunks = []
        first = 0
        for width in KEY_LOADS:
            codes = sb(f"key_codes{first}", [P, width], U32)
            nc.sync.dma_start(out=codes[:].bitcast(I32), in_=words[:, first : first + width])
            key_chunks.extend(codes[:, c : c + BANK] for c in range(0, width, BANK))
            first = first + width

        list2 = keep.tile([P, I // 16], U16, name="list2")
        nc.sync.dma_start(list2[:], offs2)
        list1 = keep.tile([P, I // 16], U16, name="list1")
        nc.sync.dma_start(list1[:], offs)
        factor_cols = sb("factor_cols", [P, PACK], F32)
        nc.sync.dma_start(out=factor_cols[:], in_=slot_factor.rearrange("o (p t) -> (o p) t", t=PACK))

        val_rows = []
        for j in range(E_TILES):
            rows = sb(f"val_rows{j}", [P, T], F32)
            nc.sync.dma_start(out=rows[:], in_=vals[j * P : (j + 1) * P, :])
            val_rows.append(rows)
        list3 = keep.tile([P, Q // 16], U16, name="list3")
        nc.sync.dma_start(list3[:], offs3)
        member_rows = {}
        for j in (1, 2, 3, 0):
            member_rows[j] = sb(f"member_rows{j}", [P, M], F32)
            nc.sync.dma_start(out=member_rows[j][:], in_=member[j * P : (j + 1) * P, :])

        key_scales = sb("key_scales", [P, BANK], U8)
        nc.vector.memset(key_scales[:].bitcast(I32), 0)
        ident = sb("ident", [P, P], F32)
        make_identity(nc, ident[:])

        q_woven = []
        for h in range(Q_TILES):
            woven = sb(f"q_woven{h}", [P, P, PACK], BF16)
            src = q_raw[:, :, h * P : (h + 1) * P].rearrange("p t (c x) -> p c t x", x=4)
            dst = woven[:].rearrange("p (c x) t -> p c t x", x=4)
            if h == 0:
                nc.vector.tensor_copy(out=dst, in_=src)
            else:
                nc.scalar.activation(out=dst, in_=src, func=ACT.Copy)
            q_woven.append(woven)
        for quad in range(4):
            live = slice(32 * quad, 32 * quad + 16)
            nc.vector.tensor_copy(out=key_scales[live, :].bitcast(I32), in_=landed[live, :])
        q_codes, q_scales = [], []
        for h in range(Q_TILES):
            codes = sb(f"q_codes{h}", [P, P], U32)
            scales = sb(f"q_scales{h}", [P, P], U8)
            nc.vector.quantize_mx(
                out=codes[:].bitcast(FP8X4), scales=scales[:], in_=q_woven[h][:].rearrange("p q t -> p (q t)")
            )
            q_codes.append(codes)
            q_scales.append(scales)

        scores = [sb(f"scores{h}", [P, T], F32) for h in range(Q_TILES)]
        for h in range(Q_TILES):
            for c in range(KEY_CHUNKS):
                acc = acc_pool.tile([P, BANK], F32, name="acc")
                nc.tensor.matmul_mx(
                    out=acc[:],
                    lhsT=q_codes[h][:].bitcast(FP8X4),
                    lhsT_scale=q_scales[h][:],
                    rhs=key_chunks[c].bitcast(FP8X4),
                    rhs_scale=key_scales[4 * c : P, :],
                    start=True,
                    stop=True,
                )
                dst = scores[h][:, c * BANK : (c + 1) * BANK]
                if c % 2 == 1:
                    nc.vector.tensor_copy(out=dst, in_=acc[:])
                else:
                    nc.scalar.copy(out=dst, in_=acc[:])

        factor_bank = acc_pool.tile([P, PACK, P], F32, name="factor_bank", tag="acc")
        for t in range(PACK):
            nc.tensor.transpose(factor_bank[:, t, :], factor_cols[:, t : t + 1].to_broadcast([P, P]), ident[:])

        def turn(rows):
            pairs = rows[:].bitcast(F32)
            bank = turn_pool.tile([P, 2, P], F32, name="turn")
            for u in range(2):
                nc.tensor.transpose(bank[:, u, :], pairs[:, u::2], ident[:])
            return bank

        def weave(copy, bank, woven):
            copy(out=woven.bitcast(F32).rearrange("p (r u) -> p r u", u=2), in_=bank[:].rearrange("p u r -> p r u"))

        def quantise(name, woven, tag=None):
            width = woven.shape[1] // PACK
            codes = sb(f"{name}_codes", [P, width], U32, tag=tag)
            scales = sb(f"{name}_scales", [P, width], U8)
            nc.vector.quantize_mx(out=codes[:].bitcast(FP8X4), scales=scales[:], in_=woven[:])
            return codes, scales

        def gather_values(j):
            rows = sb(f"v_rows{j}", [P, I], BF16)
            nc.scalar.activation(out=rows[:], in_=val_rows[j][:].indirect(list1[:]), func=ACT.Copy)
            return rows

        def difference(h):
            diff = sb(f"diff{h}", [P, I], F32)
            nc.vector.tensor_tensor(diff[:], scores[h][:].indirect(list1[:]), second[h][:], ALU.subtract)
            return diff

        def weigh(h, diff, tag=None):
            rows = sb(f"w_rows{h}", [P, I], BF16, tag=tag)
            nc.vector.scalar_tensor_tensor(
                out=rows[:].rearrange("q (p t) -> q p t", t=PACK),
                in0=diff[:].rearrange("q (p t) -> q p t", t=PACK),
                scalar=0.0,
                in1=factor_bank[:].rearrange("q t p -> q p t"),
                op0=ALU.max,
                op1=ALU.mult,
            )
            return rows

        W = P * PACK
        second0 = sb("second0", [P, I], F32)
        nc.vector.tensor_copy(out=second0[:], in_=scores[0][:].indirect(list2[:]))
        v_bank0 = turn(gather_values(0))
        second1 = sb("second1", [P, I], F32, tag="val_rows0")
        nc.scalar.activation(out=second1[:], in_=scores[1][:].indirect(list2[:]), func=ACT.Copy)
        second = [second0, second1]

        early_woven = sb("early_woven", [P, 2 * W], BF16)
        late_woven = sb("late_woven", [P, 3 * W], BF16)
        diff0 = difference(0)
        weave(nc.vector.tensor_copy, v_bank0, early_woven[:, 0:W])
        w_bank0 = turn(weigh(0, diff0, tag="v_rows0"))
        diff1 = difference(1)
        weave(nc.vector.tensor_copy, w_bank0, late_woven[:, 0:W])
        v_bank1 = turn(gather_values(1))
        w_bank1 = turn(weigh(1, diff1, tag="v_rows1"))
        weave(nc.vector.tensor_copy, v_bank1, early_woven[:, W : 2 * W])
        weave(nc.vector.tensor_copy, w_bank1, late_woven[:, W : 2 * W])
        weave(nc.vector.tensor_copy, turn(gather_values(2)), late_woven[:, 2 * W : 3 * W])
        early_codes, early_scales = quantise("early", early_woven, tag="v_rows2")
        v_bank3 = turn(gather_values(3))
        late_codes, late_scales = quantise("late", late_woven, tag="val_rows3")

        def gather_members(j):
            picked = sb(f"picked{j}", [P, Q], F32)
            nc.scalar.activation(out=picked[:], in_=member_rows[j][:].indirect(list3[:]), func=ACT.Copy)
            return picked

        picked = {1: gather_members(1)}
        v_woven3 = sb("v_woven3", [P, W], BF16, tag="member_rows1")
        weave(nc.scalar.copy, v_bank3, v_woven3[:])
        v_mx3 = quantise("v3", v_woven3)
        picked[2] = gather_members(2)
        picked[3] = gather_members(3)
        v_codes = [early_codes[:, 0:P], early_codes[:, P : 2 * P], late_codes[:, Q : Q + P], v_mx3[0][:]]
        v_scales = [early_scales[:, 0:P], early_scales[:, P : 2 * P], late_scales[:, Q : Q + P], v_mx3[1][:]]

        gaps = sb("gaps", [P, E_TILES + 1, Q], F32, tag="member_rows1")
        for j in range(E_TILES):
            acc = acc_pool.tile([P, BANK], F32, name="acc")
            nc.tensor.matmul_mx(
                out=acc[:, 0:Q],
                lhsT=v_codes[j].bitcast(FP8X4),
                lhsT_scale=v_scales[j],
                rhs=late_codes[:, 0:Q].bitcast(FP8X4),
                rhs_scale=late_scales[:, 0:Q],
                start=True,
                stop=True,
            )
            if j == 0:
                nc.vector.tensor_copy(out=gaps[:, E_TILES, :], in_=acc[:, 0:Q])
            else:
                nc.vector.tensor_tensor(gaps[:, j, :], acc[:, 0:Q], picked[j][:], ALU.subtract)
        nc.vector.tensor_tensor(gaps[:, 0, :], member_rows[0][:].indirect(list3[:]), gaps[:, E_TILES, :], ALU.subtract)

        dist = sb("dist", [P, E_TILES, Q], F32, tag="member_rows3")
        out_tiles = out.rearrange("(j p) q -> p j q", p=P)
        for tiles, queue in ((slice(1, 3), nc.sync), (slice(3, 4), nc.sync), (slice(0, 1), nc.scalar)):
            nc.scalar.activation(out=dist[:, tiles, :], in_=gaps[:, tiles, :], func=ACT.Abs)
            queue.dma_start(out=out_tiles[:, tiles, :], in_=dist[:, tiles, :])
